import numpy as np
import ml_dtypes


def mxq(x, axis, fmt="e4m3"):
    dtype, down = {"e4m3": (ml_dtypes.float8_e4m3fn, 7), "e5m2": (ml_dtypes.float8_e5m2, 14)}[fmt]
    v = np.moveaxis(np.asarray(x, np.float32).astype(ml_dtypes.bfloat16).astype(np.float64), axis, -1)
    blocks = v.reshape(v.shape[:-1] + (-1, 32))
    amax = np.abs(blocks).max(-1, keepdims=True)
    byte = np.maximum(np.where(amax > 0, np.frexp(amax)[1] - 1 + 127, 0) - down, 1)
    scale = np.exp2(byte - 127.0)
    codes = (blocks / scale).astype(np.float32).astype(dtype).astype(np.float64)
    return np.moveaxis((codes * scale).reshape(v.shape), -1, axis)


WIDE = False


def mx_kscale(k):
    if not WIDE:
        return np.ones(k)
    levels = np.array([30, -30])
    if k % 512:
        return np.exp2(np.random.permutation(np.resize(levels, k // 32))).repeat(32)
    a = np.empty((k // 512, 16))
    for p in range(k // 512):
        a[p, :8] = np.random.permutation(np.resize(levels, 8))
        for g in range(8):
            far = levels[np.abs(levels - a[p, g]) >= 10]
            a[p, g + 8] = far[np.random.randint(len(far))]
    return np.exp2(a.ravel()).repeat(32)


def f64(x):
    return np.asarray(x).astype(np.float64)


E2M1 = np.array([0.0, 0.5, 1.0, 1.5, 2.0, 3.0, 4.0, 6.0, -0.0, -0.5, -1.0, -1.5, -2.0, -3.0, -4.0, -6.0])


def pack_weight(w, fmt):
    k, n = w.shape
    w = f64(np.asarray(w, np.float32).astype(ml_dtypes.bfloat16)).reshape(k // 32, 32, n)
    amax = np.abs(w).max(1)
    if fmt == "e4m3":
        byte = np.frexp(amax)[1] - 1 + 127 - 7
    else:
        mant, ex = np.frexp(amax / 6.0)
        byte = np.where(mant > 0.5, ex, ex - 1) + 127
    byte = np.clip(np.where(amax > 0, byte, 1), 1, 254)
    scaled = (w * np.exp2(127.0 - byte)[:, None, :]).reshape(k, n).astype(np.float32)
    by_word = np.ascontiguousarray(scaled.reshape(k // 512, 128, 4, n).transpose(0, 1, 3, 2))
    if fmt == "e4m3":
        words = by_word.astype(ml_dtypes.float8_e4m3fn).view(np.uint8)
    else:
        c = by_word.astype(ml_dtypes.float4_e2m1fn).view(np.uint8) & 0xF
        words = (c[..., 0::2] | (c[..., 1::2] << 4)).reshape(k // 512, 128, 2 * n)
    return np.ascontiguousarray(words), np.ascontiguousarray(byte.astype(np.uint8).reshape(k // 512, 16, n))


def unpack_weight(words, scales, fmt):
    g, _, n = scales.shape
    words = np.ascontiguousarray(words).reshape(g, 128, n, -1)
    if fmt == "e4m3":
        vals = words.view(ml_dtypes.float8_e4m3fn).astype(np.float64)
    else:
        nib = np.empty((g, 128, n, 4), np.uint8)
        nib[..., 0::2] = words & 0xF
        nib[..., 1::2] = words >> 4
        vals = E2M1[nib]
    vals = vals * np.repeat(np.exp2(scales.astype(np.float64) - 127.0), 8, axis=1)[..., None]
    return vals.transpose(0, 1, 3, 2).reshape(g * 512, n)


O, K, M, T = 1024, 1536, 512, 1024


def setup_inputs():
    n = np.random.standard_normal
    s = mx_kscale(K)[:, None]
    dy = np.exp(0.5 * n((1, T))) * n((K, T))
    w = n((K, M)) / np.sqrt(K) / s
    p_w8 = pack_weight(w[:O], "e4m3")
    p_w4 = pack_weight(w[O:], "e2m1")
    return {
        "dy": (dy * s).astype(np.float32),
        "w8_words": p_w8[0],
        "w8_scales": p_w8[1],
        "w4_words": p_w4[0],
        "w4_scales": p_w4[1],
        "r": (n((512, 1024))).astype(np.float32),
    }


def reference(dy, w8_words, w8_scales, w4_words, w4_scales, r):
    dy_ = mxq(f64(dy), 0, "e5m2")
    w8_ = unpack_weight(w8_words, w8_scales, "e4m3")
    w4_ = unpack_weight(w4_words, w4_scales, "e2m1")
    y = w8_.T @ dy_[:O] + w4_.T @ dy_[O:]
    return f64(r) + y

@@ -1,0 +1,119 @@
+from contextlib import ExitStack
+
+import concourse.mybir as mybir
+
+O, K, M, T = 1024, 1536, 512, 1024
+FLOPS = 2 * K * M * T
+
+F32 = mybir.dt.float32
+BF16 = mybir.dt.bfloat16
+I32 = mybir.dt.int32
+U32 = mybir.dt.uint32
+U8 = mybir.dt.uint8
+E4M3X4 = mybir.dt.float8_e4m3fn_x4
+E5M2X4 = mybir.dt.float8_e5m2_x4
+E2M1X4 = mybir.dt.float4_e2m1fn_x4
+ADD = mybir.AluOpType.add
+
+P = 128
+PACK = 4
+K_PASS = P * PACK
+W8_PASSES = O // K_PASS
+PASSES = K // K_PASS
+N = 512
+HALVES = T // N
+D_TILES = M // P
+V_COLS = 384
+Q_COLS = 256
+
+
+def tile_mix_dyq_fm_res_kernel(tc, dy, w8_words, w8_scales, w4_words, w4_scales, r, out):
+    nc = tc.nc
+    with ExitStack() as ctx:
+        keep = ctx.enter_context(tc.tile_pool(name="keep", bufs=1))
+        psum = ctx.enter_context(tc.psum_pool(name="psum", bufs=1))
+        ctx.enter_context(tc.manual_schedule())
+
+        ws = keep.tile([P, PASSES, M], U8, name="ws", align_bytes=64)
+        nc.gpsimd.memset(ws[:].rearrange("p a n -> p (a n)").bitcast(I32), 0)
+        for q in range(4):
+            nc.gpsimd.dma_start(
+                out=ws[32 * q : 32 * q + 4, 0:W8_PASSES, :].bitcast(I32),
+                in_=w8_scales[:, 4 * q : 4 * q + 4, :].rearrange("a q n -> q a n").bitcast(I32),
+            )
+        for q in range(4):
+            nc.gpsimd.dma_start(
+                out=ws[32 * q : 32 * q + 4, W8_PASSES, :].bitcast(I32),
+                in_=w4_scales[0, 4 * q : 4 * q + 4, :].bitcast(I32),
+            )
+
+        w8 = keep.tile([P, W8_PASSES, M], I32, name="w8", align_bytes=64)
+        w4 = keep.tile([P, 2 * M], U8, name="w4", align_bytes=64)
+        raw = {}
+
+        def load_dy(g, t0, width):
+            tile = keep.tile([P, PACK, width], F32, name=f"raw_{g}_{t0}", align_bytes=64)
+            rows = dy[g * K_PASS : (g + 1) * K_PASS, :].rearrange("(p i) t -> p i t", i=PACK)
+            nc.sync.dma_start(out=tile[:], in_=rows[:, :, t0 : t0 + width])
+            for h in range(t0 // N, (t0 + width) // N):
+                raw[g, h] = (tile, h * N - t0)
+
+        load_dy(0, 0, T)
+        nc.sync.dma_start(out=w8[:], in_=w8_words.rearrange("a p d i -> p a (d i)").bitcast(I32))
+        load_dy(1, 0, T)
+        load_dy(2, 0, N)
+        nc.sync.dma_start(out=w4[:].bitcast(I32), in_=w4_words[0].bitcast(I32))
+        load_dy(2, N, N)
+        res = []
+        for d in range(D_TILES):
+            tile = keep.tile([P, T], F32, name=f"res_{d}", align_bytes=64)
+            nc.sync.dma_start(out=tile[:], in_=r[d * P : (d + 1) * P, :])
+            res.append(tile)
+
+        acc = {}
+        for h in range(HALVES):
+            for d in range(D_TILES):
+                acc[d, h] = psum.tile([P, N], F32, name=f"acc_{d}_{h}")
+
+        for g in range(PASSES):
+            for h in range(HALVES):
+                tile, t0 = raw[g, h]
+                grouped = keep.tile([P, N, PACK], BF16, name=f"grouped_{g}_{h}", align_bytes=64)
+                codes = keep.tile([P, N], U32, name=f"codes_{g}_{h}", align_bytes=64)
+                scales = keep.tile([P, N], U8, name=f"scales_{g}_{h}", align_bytes=64)
+
+                def copy(engine_copy, a, b):
+                    engine_copy(
+                        out=grouped[:, a:b, :].rearrange("p (c n) i -> p c i n", n=4),
+                        in_=tile[:, :, t0 + a : t0 + b].rearrange("p i (c n) -> p c i n", n=4),
+                    )
+
+                copy(nc.scalar.copy, V_COLS, N)
+                copy(nc.vector.tensor_copy, 0, Q_COLS)
+                copy(nc.vector.tensor_copy, Q_COLS, V_COLS)
+                for a in range(0, N, Q_COLS):
+                    nc.vector.quantize_mx(
+                        out=codes[:, a : a + Q_COLS].bitcast(E5M2X4),
+                        scales=scales[:, a : a + Q_COLS],
+                        in_=grouped[:, a : a + Q_COLS, :].rearrange("p t i -> p (t i)"),
+                    )
+                for d in range(D_TILES):
+                    if g < W8_PASSES:
+                        lhsT = w8[:, g, d * P : (d + 1) * P].bitcast(E4M3X4)
+                    else:
+                        lhsT = w4[:, 2 * d * P : 2 * (d + 1) * P].bitcast(E2M1X4)
+                    nc.tensor.matmul_mx(
+                        out=acc[d, h][:],
+                        lhsT=lhsT,
+                        lhsT_scale=ws[:, g, d * P : (d + 1) * P],
+                        rhs=codes[:].bitcast(E5M2X4),
+                        rhs_scale=scales[:],
+                        start=(g == 0),
+                        stop=(g == PASSES - 1),
+                    )
+
+        for d, h in ((0, 0), (1, 0), (0, 1), (1, 1), (2, 0), (2, 1), (3, 0), (3, 1)):
+            o = keep.tile([P, N], F32, name=f"o_{d}_{h}", align_bytes=64)
+            cols = slice(h * N, (h + 1) * N)
+            nc.vector.tensor_tensor(out=o[:], in0=acc[d, h][:], in1=res[d][:, cols], op=ADD)
+            nc.sync.dma_start(out=out[d * P : (d + 1) * P, cols], in_=o[:])

@@ -23,7 +23,7 @@ PASSES = K // K_PASS
 N = 512
 HALVES = T // N
 D_TILES = M // P
-V_COLS = 384
+V_COLS = 320
 Q_COLS = 256
 
 
@@ -62,8 +62,8 @@ def tile_mix_dyq_fm_res_kernel(tc, dy, w8_words, w8_scales, w4_words, w4_scales,
         nc.sync.dma_start(out=w8[:], in_=w8_words.rearrange("a p d i -> p a (d i)").bitcast(I32))
         load_dy(1, 0, T)
         load_dy(2, 0, N)
-        nc.sync.dma_start(out=w4[:].bitcast(I32), in_=w4_words[0].bitcast(I32))
         load_dy(2, N, N)
+        nc.sync.dma_start(out=w4[:].bitcast(I32), in_=w4_words[0].bitcast(I32))
         res = []
         for d in range(D_TILES):
             tile = keep.tile([P, T], F32, name=f"res_{d}", align_bytes=64)
@@ -112,8 +112,12 @@ def tile_mix_dyq_fm_res_kernel(tc, dy, w8_words, w8_scales, w4_words, w4_scales,
                         stop=(g == PASSES - 1),
                     )
 
+        sums = [keep.tile([P, T], F32, name=f"sum_{d}", align_bytes=64) for d in range(D_TILES)]
+        queues = (nc.sync, nc.scalar)
         for d, h in ((0, 0), (1, 0), (0, 1), (1, 1), (2, 0), (2, 1), (3, 0), (3, 1)):
-            o = keep.tile([P, N], F32, name=f"o_{d}_{h}", align_bytes=64)
             cols = slice(h * N, (h + 1) * N)
-            nc.vector.tensor_tensor(out=o[:], in0=acc[d, h][:], in1=res[d][:, cols], op=ADD)
-            nc.sync.dma_start(out=out[d * P : (d + 1) * P, cols], in_=o[:])
+            nc.vector.tensor_tensor(out=sums[d][:, cols], in0=acc[d, h][:], in1=res[d][:, cols], op=ADD)
+            if d < 2:
+                queues[d % 2].dma_start(out=out[d * P : (d + 1) * P, cols], in_=sums[d][:, cols])
+            elif h == HALVES - 1:
+                queues[d % 2].dma_start(out=out[d * P : (d + 1) * P, :], in_=sums[d][:])

from contextlib import ExitStack

import concourse.mybir as mybir

O, K, M, T = 1024, 1536, 512, 1024
FLOPS = 2 * K * M * T

F32 = mybir.dt.float32
BF16 = mybir.dt.bfloat16
I32 = mybir.dt.int32
U32 = mybir.dt.uint32
U8 = mybir.dt.uint8
E4M3X4 = mybir.dt.float8_e4m3fn_x4
E5M2X4 = mybir.dt.float8_e5m2_x4
E2M1X4 = mybir.dt.float4_e2m1fn_x4
ADD = mybir.AluOpType.add

P = 128
PACK = 4
K_PASS = P * PACK
W8_PASSES = O // K_PASS
PASSES = K // K_PASS
N = 512
HALVES = T // N
D_TILES = M // P
V_COLS = 320
Q_COLS = 256


def tile_mix_dyq_fm_res_kernel(tc, dy, w8_words, w8_scales, w4_words, w4_scales, r, out):
    nc = tc.nc
    with ExitStack() as ctx:
        keep = ctx.enter_context(tc.tile_pool(name="keep", bufs=1))
        psum = ctx.enter_context(tc.psum_pool(name="psum", bufs=1))
        ctx.enter_context(tc.manual_schedule())

        ws = keep.tile([P, PASSES, M], U8, name="ws", align_bytes=64)
        nc.gpsimd.memset(ws[:].rearrange("p a n -> p (a n)").bitcast(I32), 0)
        for q in range(4):
            nc.gpsimd.dma_start(
                out=ws[32 * q : 32 * q + 4, 0:W8_PASSES, :].bitcast(I32),
                in_=w8_scales[:, 4 * q : 4 * q + 4, :].rearrange("a q n -> q a n").bitcast(I32),
            )
        for q in range(4):
            nc.gpsimd.dma_start(
                out=ws[32 * q : 32 * q + 4, W8_PASSES, :].bitcast(I32),
                in_=w4_scales[0, 4 * q : 4 * q + 4, :].bitcast(I32),
            )

        w8 = keep.tile([P, W8_PASSES, M], I32, name="w8", align_bytes=64)
        w4 = keep.tile([P, 2 * M], U8, name="w4", align_bytes=64)
        raw = {}

        def load_dy(g, t0, width):
            tile = keep.tile([P, PACK, width], F32, name=f"raw_{g}_{t0}", align_bytes=64)
            rows = dy[g * K_PASS : (g + 1) * K_PASS, :].rearrange("(p i) t -> p i t", i=PACK)
            nc.sync.dma_start(out=tile[:], in_=rows[:, :, t0 : t0 + width])
            for h in range(t0 // N, (t0 + width) // N):
                raw[g, h] = (tile, h * N - t0)

        load_dy(0, 0, T)
        nc.sync.dma_start(out=w8[:], in_=w8_words.rearrange("a p d i -> p a (d i)").bitcast(I32))
        load_dy(1, 0, T)
        load_dy(2, 0, N)
        load_dy(2, N, N)
        nc.sync.dma_start(out=w4[:].bitcast(I32), in_=w4_words[0].bitcast(I32))
        res = []
        for d in range(D_TILES):
            tile = keep.tile([P, T], F32, name=f"res_{d}", align_bytes=64)
            nc.sync.dma_start(out=tile[:], in_=r[d * P : (d + 1) * P, :])
            res.append(tile)

        acc = {}
        for h in range(HALVES):
            for d in range(D_TILES):
                acc[d, h] = psum.tile([P, N], F32, name=f"acc_{d}_{h}")

        for g in range(PASSES):
            for h in range(HALVES):
                tile, t0 = raw[g, h]
                grouped = keep.tile([P, N, PACK], BF16, name=f"grouped_{g}_{h}", align_bytes=64)
                codes = keep.tile([P, N], U32, name=f"codes_{g}_{h}", align_bytes=64)
                scales = keep.tile([P, N], U8, name=f"scales_{g}_{h}", align_bytes=64)

                def copy(engine_copy, a, b):
                    engine_copy(
                        out=grouped[:, a:b, :].rearrange("p (c n) i -> p c i n", n=4),
                        in_=tile[:, :, t0 + a : t0 + b].rearrange("p i (c n) -> p c i n", n=4),
                    )

                copy(nc.scalar.copy, V_COLS, N)
                copy(nc.vector.tensor_copy, 0, Q_COLS)
                copy(nc.vector.tensor_copy, Q_COLS, V_COLS)
                for a in range(0, N, Q_COLS):
                    nc.vector.quantize_mx(
                        out=codes[:, a : a + Q_COLS].bitcast(E5M2X4),
                        scales=scales[:, a : a + Q_COLS],
                        in_=grouped[:, a : a + Q_COLS, :].rearrange("p t i -> p (t i)"),
                    )
                for d in range(D_TILES):
                    if g < W8_PASSES:
                        lhsT = w8[:, g, d * P : (d + 1) * P].bitcast(E4M3X4)
                    else:
                        lhsT = w4[:, 2 * d * P : 2 * (d + 1) * P].bitcast(E2M1X4)
                    nc.tensor.matmul_mx(
                        out=acc[d, h][:],
                        lhsT=lhsT,
                        lhsT_scale=ws[:, g, d * P : (d + 1) * P],
                        rhs=codes[:].bitcast(E5M2X4),
                        rhs_scale=scales[:],
                        start=(g == 0),
                        stop=(g == PASSES - 1),
                    )

        sums = [keep.tile([P, T], F32, name=f"sum_{d}", align_bytes=64) for d in range(D_TILES)]
        queues = (nc.sync, nc.scalar)
        for d, h in ((0, 0), (1, 0), (0, 1), (1, 1), (2, 0), (2, 1), (3, 0), (3, 1)):
            cols = slice(h * N, (h + 1) * N)
            nc.vector.tensor_tensor(out=sums[d][:, cols], in0=acc[d, h][:], in1=res[d][:, cols], op=ADD)
            if d < 2:
                queues[d % 2].dma_start(out=out[d * P : (d + 1) * P, cols], in_=sums[d][:, cols])
            elif h == HALVES - 1:
                queues[d % 2].dma_start(out=out[d * P : (d + 1) * P, :], in_=sums[d][:])
